import numpy as np
import ml_dtypes


def mxq(x, axis, fmt="e4m3"):
    dtype, down = {"e4m3": (ml_dtypes.float8_e4m3fn, 7), "e5m2": (ml_dtypes.float8_e5m2, 14)}[fmt]
    v = np.moveaxis(np.asarray(x, np.float32).astype(ml_dtypes.bfloat16).astype(np.float64), axis, -1)
    blocks = v.reshape(v.shape[:-1] + (-1, 32))
    amax = np.abs(blocks).max(-1, keepdims=True)
    byte = np.maximum(np.where(amax > 0, np.frexp(amax)[1] - 1 + 127, 0) - down, 1)
    scale = np.exp2(byte - 127.0)
    codes = (blocks / scale).astype(np.float32).astype(dtype).astype(np.float64)
    return np.moveaxis((codes * scale).reshape(v.shape), -1, axis)


WIDE = False


def mx_kscale(k):
    if not WIDE:
        return np.ones(k)
    levels = np.array([10, -10, 5, -5, 0])
    if k % 512:
        return np.exp2(np.random.permutation(np.resize(levels, k // 32))).repeat(32)
    a = np.empty((k // 512, 16))
    for p in range(k // 512):
        a[p, :8] = np.random.permutation(np.resize(levels, 8))
        for g in range(8):
            far = levels[np.abs(levels - a[p, g]) >= 10]
            a[p, g + 8] = far[np.random.randint(len(far))]
    return np.exp2(a.ravel()).repeat(32)


def f64(x):
    return np.asarray(x).astype(np.float64)


def striped(idx):
    return np.tile(idx.reshape(-1, 16).T, (8, 1)).astype(np.uint16)


def unstriped(offs):
    return offs[:16].T.reshape(-1).astype(np.int64)


def gelu(v):
    return 0.5 * v * (1.0 + np.tanh(np.sqrt(2.0 / np.pi) * (v + 0.044715 * v**3)))


K, T, E, C, N = 1024, 1024, 8, 128, 384


def by_expert(wq, xq):
    return np.concatenate([wq[e].T @ xq[:, e * C:(e + 1) * C] for e in range(E)], axis=1)


def setup_inputs():
    n = np.random.standard_normal
    s = mx_kscale(K)[:, None]
    return {
        "xT": (n((K, T)) * s).astype(np.float32),
        "w": (n((E, K, N)) / np.sqrt(K) / s[None]).astype(np.float32),
        "b": (0.3 * n((N, E))).astype(np.float32),
        "gate": np.tile(np.random.uniform(0.2, 1.0, E * C), (N, 1)).astype(np.float32),
        "offs": striped(np.random.permutation(T)[:E * C]),
        "dst": striped(np.random.permutation(T)[:E * C]),
    }


def reference(xT, w, b, gate, offs, dst):
    idx = unstriped(offs)
    xq = mxq(f64(xT)[:, idx], 0, "e4m3")
    y = by_expert(mxq(f64(w), 1, "e4m3"), xq)
    y = gelu(y + np.repeat(f64(b), C, axis=1))
    out = np.zeros((N, T))
    out[:, unstriped(dst)] = f64(gate) * y
    return out

@@ -1,0 +1,189 @@
+from contextlib import ExitStack
+
+import concourse.mybir as mybir
+
+K, T, E, C, N = 1024, 1024, 8, 128, 384
+FLOPS = 2 * K * N * E * C
+
+F32 = mybir.dt.float32
+BF16 = mybir.dt.bfloat16
+U32 = mybir.dt.uint32
+I32 = mybir.dt.int32
+U16 = mybir.dt.uint16
+U8 = mybir.dt.uint8
+FP8X4 = mybir.dt.float8_e4m3fn_x4
+COPY = mybir.ActivationFunctionType.Copy
+GELU = mybir.ActivationFunctionType.Gelu_apprx_tanh
+MULT = mybir.AluOpType.mult
+
+P = 128
+J = 4
+PASSES = 2
+ROWS = 512
+NT = N // P
+HALF = 512
+GROUPS = ((0, 1), (2, 3), (4, 5), (6,), (7,))
+
+
+def tile_moe_two_lin_gelu_kernel(tc, xT, w, b, gate, offs, dst, out):
+    nc = tc.nc
+    with ExitStack() as ctx:
+        keep = ctx.enter_context(tc.tile_pool(name="keep", bufs=1))
+        xraw_pool = ctx.enter_context(tc.tile_pool(name="xraw", bufs=4))
+        xbf_pool = ctx.enter_context(tc.tile_pool(name="xbf", bufs=4))
+        wraw_pool = ctx.enter_context(tc.tile_pool(name="wraw", bufs=14))
+        wbf_pool = ctx.enter_context(tc.tile_pool(name="wbf", bufs=3))
+        wq_pool = ctx.enter_context(tc.tile_pool(name="wq", bufs=4))
+        y_pool = ctx.enter_context(tc.tile_pool(name="y", bufs=6))
+        psum = ctx.enter_context(tc.psum_pool(name="psum", bufs=8))
+
+        src_list = keep.tile([P, E * C // 16], U16, name="src_list")
+        dst_list = keep.tile([P, E * C // 16], U16, name="dst_list")
+        x_words = [keep.tile([P, T], U32, name=f"x_words{a}", align_bytes=64) for a in range(PASSES)]
+        x_bytes = keep.tile([P, T], U8, name="x_bytes", align_bytes=64)
+        gate_sb = keep.tile([P, E * C], F32, name="gate_sb")
+        bias = keep.tile([P, NT, E], F32, name="bias")
+        warm = keep.tile([P, 1], F32, name="warm")
+        warm_out = keep.tile([P, 1], F32, name="warm_out")
+        outs = [keep.tile([P, T], F32, name=f"placed{n}") for n in range(NT)]
+        g_words = [[keep.tile([P, HALF], U32, name=f"g_words{a}{h}", align_bytes=64) for h in range(2)] for a in range(PASSES)]
+        g_bytes = [keep.tile([P, HALF], U8, name=f"g_bytes{h}", align_bytes=64) for h in range(2)]
+
+        x_raw = {}
+        w_raw = {}
+
+        def load_x(a, h):
+            raw = xraw_pool.tile([P, J, HALF], F32, name="raw_x")
+            nc.sync.dma_start(
+                out=raw[:],
+                in_=xT[a * ROWS : (a + 1) * ROWS, h * HALF : (h + 1) * HALF].rearrange("(p j) t -> p j t", j=J),
+            )
+            x_raw[a, h] = raw
+
+        def load_w(e, a):
+            raw = wraw_pool.tile([P, J, N], F32, name="raw_w")
+            nc.sync.dma_start(out=raw[:], in_=w[e, a * ROWS : (a + 1) * ROWS, :].rearrange("(p j) n -> p j n", j=J))
+            w_raw[e, a] = raw
+
+        nc.vector.memset(warm[:], 0.0)
+        nc.scalar.activation(warm_out[:], warm[:], GELU)
+        nc.vector.memset(x_bytes[:].bitcast(I32), 0)
+        nc.scalar.dma_start(out=bias[:], in_=b.rearrange("(t p) e -> p t e", p=P))
+
+        load_x(0, 0)
+        load_x(0, 1)
+        nc.sync.dma_start(src_list[:], offs)
+        load_x(1, 0)
+        load_x(1, 1)
+        load_w(0, 0)
+        load_w(0, 1)
+        nc.sync.dma_start(dst_list[:], dst)
+        load_w(1, 0)
+        load_w(1, 1)
+        nc.sync.dma_start(out=gate_sb[:], in_=gate[0:P, :])
+        for e in range(2, E):
+            load_w(e, 0)
+            load_w(e, 1)
+
+        def interleave(engine, dst_ap, src_ap):
+            o = dst_ap.rearrange("p (c i) j -> p c j i", i=4)
+            i = src_ap.rearrange("p j (c i) -> p c j i", i=4)
+            if engine == "v":
+                nc.vector.tensor_copy(o, i)
+            else:
+                nc.scalar.activation(o, i, COPY)
+
+        def x_half(a, h, engines):
+            for s, engine in enumerate(engines):
+                cols = slice(s * 256, (s + 1) * 256)
+                bf = xbf_pool.tile([P, 256, J], BF16, name="bf_x", align_bytes=64)
+                interleave(engine, bf[:], x_raw[a, h][:, :, cols])
+                tok = slice(h * HALF + s * 256, h * HALF + (s + 1) * 256)
+                nc.vector.quantize_mx(
+                    out=x_words[a][:, tok].bitcast(FP8X4),
+                    scales=x_bytes[J * a : P, tok],
+                    in_=bf[:].rearrange("p c j -> p (c j)"),
+                )
+
+        def gather_words(a, h):
+            nc.vector.tensor_copy(g_words[a][h][:], x_words[a][:].indirect(src_list[:, 32 * h : 32 * (h + 1)]))
+
+        def gather_bytes(h):
+            nc.vector.tensor_copy(g_bytes[h][:], x_bytes[:].indirect(src_list[:, 32 * h : 32 * (h + 1)]))
+
+        w_bf = {}
+        w_q = {}
+
+        def copy_w(e):
+            bf = wbf_pool.tile([P, PASSES * N, J], BF16, name="bf_w", align_bytes=64)
+            for a in range(PASSES):
+                interleave("s", bf[:, a * N : (a + 1) * N, :], w_raw[e, a][:])
+            w_bf[e] = bf
+
+        def quant_w(e):
+            words = wq_pool.tile([P, PASSES * N], U32, name="words_w", align_bytes=64)
+            bytes_w = wq_pool.tile([P, PASSES * N], U8, name="bytes_w", align_bytes=64)
+            flat = w_bf[e][:].rearrange("p c j -> p (c j)")
+            for lo, hi in ((0, 512), (512, 768)):
+                nc.vector.quantize_mx(
+                    out=words[:, lo:hi].bitcast(FP8X4), scales=bytes_w[:, lo:hi], in_=flat[:, J * lo : J * hi]
+                )
+            w_q[e] = (words, bytes_w)
+
+        ys = {}
+
+        def expert(e):
+            words, bytes_w = w_q[e]
+            h, c0 = (e * C) // HALF, (e * C) % HALF
+            for n in range(NT):
+                acc = psum.tile([P, C], F32, name="acc")
+                for a in range(PASSES):
+                    col = slice(a * N + n * P, a * N + (n + 1) * P)
+                    nc.tensor.matmul_mx(
+                        out=acc[:],
+                        lhsT=words[:, col].bitcast(FP8X4),
+                        lhsT_scale=bytes_w[:, col],
+                        rhs=g_words[a][h][:, c0 : c0 + C].bitcast(FP8X4),
+                        rhs_scale=g_bytes[h][J * a : P, c0 : c0 + C],
+                        start=(a == 0),
+                        stop=(a == PASSES - 1),
+                    )
+                for group in GROUPS:
+                    if e in group:
+                        if e == group[0]:
+                            ys[group, n] = y_pool.tile([P, 256], F32, name="y")
+                        lo = (e - group[0]) * C
+                        nc.scalar.activation(ys[group, n][:, lo : lo + C], acc[:], GELU, bias=bias[:, n, e : e + 1])
+
+        def scatter(group, n):
+            lo, hi = group[0] * C, (group[-1] + 1) * C
+            nc.vector.tensor_tensor(
+                outs[n][:].indirect(dst_list[:, lo // 16 : hi // 16]), ys[group, n][:, : hi - lo], gate_sb[:, lo:hi], MULT
+            )
+
+        x_half(0, 0, "vs")
+        x_half(0, 1, "vs")
+        gather_words(0, 0)
+        x_half(1, 0, "vs")
+        x_half(1, 1, "vs")
+        copy_w(0)
+        gather_words(1, 0)
+        gather_bytes(0)
+        quant_w(0)
+        copy_w(1)
+        gather_words(0, 1)
+        for e in range(E):
+            if e + 2 < E:
+                copy_w(e + 2)
+            if e + 1 < E:
+                quant_w(e + 1)
+            expert(e)
+            if e == 1:
+                gather_words(1, 1)
+                gather_bytes(1)
+            for group in GROUPS:
+                if e == group[-1]:
+                    for n in range(NT):
+                        scatter(group, n)
+                        if e == E - 1:
+                            nc.sync.dma_start(out=out[n * P : (n + 1) * P, :], in_=outs[n][:])

@@ -22,19 +22,18 @@ PASSES = 2
 ROWS = 512
 NT = N // P
 HALF = 512
-GROUPS = ((0, 1), (2, 3), (4, 5), (6,), (7,))
+GROUPS = tuple((e,) for e in range(E))
 
 
 def tile_moe_two_lin_gelu_kernel(tc, xT, w, b, gate, offs, dst, out):
     nc = tc.nc
     with ExitStack() as ctx:
         keep = ctx.enter_context(tc.tile_pool(name="keep", bufs=1))
-        xraw_pool = ctx.enter_context(tc.tile_pool(name="xraw", bufs=4))
-        xbf_pool = ctx.enter_context(tc.tile_pool(name="xbf", bufs=4))
+        xbf_pool = ctx.enter_context(tc.tile_pool(name="xbf", bufs=8))
         wraw_pool = ctx.enter_context(tc.tile_pool(name="wraw", bufs=14))
-        wbf_pool = ctx.enter_context(tc.tile_pool(name="wbf", bufs=3))
+        wbf_pool = ctx.enter_context(tc.tile_pool(name="wbf", bufs=4))
         wq_pool = ctx.enter_context(tc.tile_pool(name="wq", bufs=4))
-        y_pool = ctx.enter_context(tc.tile_pool(name="y", bufs=6))
+        y_pool = ctx.enter_context(tc.tile_pool(name="y", bufs=9))
         psum = ctx.enter_context(tc.psum_pool(name="psum", bufs=8))
 
         src_list = keep.tile([P, E * C // 16], U16, name="src_list")
@@ -52,13 +51,14 @@ def tile_moe_two_lin_gelu_kernel(tc, xT, w, b, gate, offs, dst, out):
         x_raw = {}
         w_raw = {}
 
-        def load_x(a, h):
-            raw = xraw_pool.tile([P, J, HALF], F32, name="raw_x")
+        def load_x(a, lo, width):
+            raw = keep.tile([P, J, width], F32, name=f"raw_x{a}_{lo}")
             nc.sync.dma_start(
                 out=raw[:],
-                in_=xT[a * ROWS : (a + 1) * ROWS, h * HALF : (h + 1) * HALF].rearrange("(p j) t -> p j t", j=J),
+                in_=xT[a * ROWS : (a + 1) * ROWS, lo : lo + width].rearrange("(p j) t -> p j t", j=J),
             )
-            x_raw[a, h] = raw
+            for b in range(lo // 256, (lo + width) // 256):
+                x_raw[a, b] = raw[:, :, b * 256 - lo : (b + 1) * 256 - lo]
 
         def load_w(e, a):
             raw = wraw_pool.tile([P, J, N], F32, name="raw_w")
@@ -70,20 +70,31 @@ def tile_moe_two_lin_gelu_kernel(tc, xT, w, b, gate, offs, dst, out):
         nc.vector.memset(x_bytes[:].bitcast(I32), 0)
         nc.scalar.dma_start(out=bias[:], in_=b.rearrange("(t p) e -> p t e", p=P))
 
-        load_x(0, 0)
-        load_x(0, 1)
+        load_x(0, 0, 256)
+        load_x(0, 256, 256)
+        load_x(0, 512, 512)
         nc.sync.dma_start(src_list[:], offs)
-        load_x(1, 0)
-        load_x(1, 1)
+        load_x(1, 0, 512)
+        load_x(1, 512, 256)
+        load_x(1, 768, 256)
         load_w(0, 0)
         load_w(0, 1)
         nc.sync.dma_start(dst_list[:], dst)
         load_w(1, 0)
         load_w(1, 1)
         nc.sync.dma_start(out=gate_sb[:], in_=gate[0:P, :])
-        for e in range(2, E):
-            load_w(e, 0)
-            load_w(e, 1)
+        load_w(2, 0)
+        load_w(2, 1)
+        load_w(3, 0)
+        load_w(3, 1)
+        load_w(4, 0)
+        load_w(4, 1)
+        load_w(5, 0)
+        load_w(5, 1)
+        load_w(6, 0)
+        load_w(6, 1)
+        load_w(7, 0)
+        load_w(7, 1)
 
         def interleave(engine, dst_ap, src_ap):
             o = dst_ap.rearrange("p (c i) j -> p c j i", i=4)
@@ -93,17 +104,15 @@ def tile_moe_two_lin_gelu_kernel(tc, xT, w, b, gate, offs, dst, out):
             else:
                 nc.scalar.activation(o, i, COPY)
 
-        def x_half(a, h, engines):
-            for s, engine in enumerate(engines):
-                cols = slice(s * 256, (s + 1) * 256)
-                bf = xbf_pool.tile([P, 256, J], BF16, name="bf_x", align_bytes=64)
-                interleave(engine, bf[:], x_raw[a, h][:, :, cols])
-                tok = slice(h * HALF + s * 256, h * HALF + (s + 1) * 256)
-                nc.vector.quantize_mx(
-                    out=x_words[a][:, tok].bitcast(FP8X4),
-                    scales=x_bytes[J * a : P, tok],
-                    in_=bf[:].rearrange("p c j -> p (c j)"),
-                )
+        def x_block(a, b, engine):
+            bf = xbf_pool.tile([P, 256, J], BF16, name="bf_x", align_bytes=64)
+            interleave(engine, bf[:], x_raw[a, b])
+            tok = slice(b * 256, (b + 1) * 256)
+            nc.vector.quantize_mx(
+                out=x_words[a][:, tok].bitcast(FP8X4),
+                scales=x_bytes[J * a : P, tok],
+                in_=bf[:].rearrange("p c j -> p (c j)"),
+            )
 
         def gather_words(a, h):
             nc.vector.tensor_copy(g_words[a][h][:], x_words[a][:].indirect(src_list[:, 32 * h : 32 * (h + 1)]))
@@ -117,7 +126,7 @@ def tile_moe_two_lin_gelu_kernel(tc, xT, w, b, gate, offs, dst, out):
         def copy_w(e):
             bf = wbf_pool.tile([P, PASSES * N, J], BF16, name="bf_w", align_bytes=64)
             for a in range(PASSES):
-                interleave("s", bf[:, a * N : (a + 1) * N, :], w_raw[e, a][:])
+                interleave("v" if (e, a) in ((1, 1), (4, 1), (3, 0),) else "s", bf[:, a * N : (a + 1) * N, :], w_raw[e, a][:])
             w_bf[e] = bf
 
         def quant_w(e):
@@ -161,24 +170,27 @@ def tile_moe_two_lin_gelu_kernel(tc, xT, w, b, gate, offs, dst, out):
                 outs[n][:].indirect(dst_list[:, lo // 16 : hi // 16]), ys[group, n][:, : hi - lo], gate_sb[:, lo:hi], MULT
             )
 
-        x_half(0, 0, "vs")
-        x_half(0, 1, "vs")
+        x_block(0, 0, "s")
+        x_block(0, 1, "v")
+        x_block(0, 2, "s")
+        x_block(0, 3, "v")
         gather_words(0, 0)
-        x_half(1, 0, "vs")
-        x_half(1, 1, "vs")
+        x_block(1, 0, "s")
+        x_block(1, 1, "s")
+        x_block(1, 2, "v")
+        x_block(1, 3, "s")
         copy_w(0)
+        gather_words(0, 1)
         gather_words(1, 0)
         gather_bytes(0)
         quant_w(0)
-        copy_w(1)
-        gather_words(0, 1)
         for e in range(E):
-            if e + 2 < E:
-                copy_w(e + 2)
+            if e + 1 < E:
+                copy_w(e + 1)
             if e + 1 < E:
                 quant_w(e + 1)
             expert(e)
-            if e == 1:
+            if e == 2:
                 gather_words(1, 1)
                 gather_bytes(1)
             for group in GROUPS:

@@ -22,7 +22,6 @@ PASSES = 2
 ROWS = 512
 NT = N // P
 HALF = 512
-GROUPS = tuple((e,) for e in range(E))
 
 
 def tile_moe_two_lin_gelu_kernel(tc, xT, w, b, gate, offs, dst, out):
@@ -33,7 +32,7 @@ def tile_moe_two_lin_gelu_kernel(tc, xT, w, b, gate, offs, dst, out):
         wraw_pool = ctx.enter_context(tc.tile_pool(name="wraw", bufs=14))
         wbf_pool = ctx.enter_context(tc.tile_pool(name="wbf", bufs=4))
         wq_pool = ctx.enter_context(tc.tile_pool(name="wq", bufs=4))
-        y_pool = ctx.enter_context(tc.tile_pool(name="y", bufs=9))
+        y_pool = ctx.enter_context(tc.tile_pool(name="y", bufs=4))
         psum = ctx.enter_context(tc.psum_pool(name="psum", bufs=8))
 
         src_list = keep.tile([P, E * C // 16], U16, name="src_list")
@@ -68,7 +67,6 @@ def tile_moe_two_lin_gelu_kernel(tc, xT, w, b, gate, offs, dst, out):
         nc.vector.memset(warm[:], 0.0)
         nc.scalar.activation(warm_out[:], warm[:], GELU)
         nc.vector.memset(x_bytes[:].bitcast(I32), 0)
-        nc.scalar.dma_start(out=bias[:], in_=b.rearrange("(t p) e -> p t e", p=P))
 
         load_x(0, 0, 256)
         load_x(0, 256, 256)
@@ -80,6 +78,7 @@ def tile_moe_two_lin_gelu_kernel(tc, xT, w, b, gate, offs, dst, out):
         load_w(0, 0)
         load_w(0, 1)
         nc.sync.dma_start(dst_list[:], dst)
+        nc.sync.dma_start(out=bias[:], in_=b.rearrange("(t p) e -> p t e", p=P))
         load_w(1, 0)
         load_w(1, 1)
         nc.sync.dma_start(out=gate_sb[:], in_=gate[0:P, :])
@@ -157,18 +156,20 @@ def tile_moe_two_lin_gelu_kernel(tc, xT, w, b, gate, offs, dst, out):
                         start=(a == 0),
                         stop=(a == PASSES - 1),
                     )
-                for group in GROUPS:
-                    if e in group:
-                        if e == group[0]:
-                            ys[group, n] = y_pool.tile([P, 256], F32, name="y")
-                        lo = (e - group[0]) * C
-                        nc.scalar.activation(ys[group, n][:, lo : lo + C], acc[:], GELU, bias=bias[:, n, e : e + 1])
+                if n == 0:
+                    ys[e] = y_pool.tile([P, NT, C], F32, name="y")
+                nc.scalar.activation(ys[e][:, n, :], acc[:], GELU, bias=bias[:, n, e : e + 1])
 
-        def scatter(group, n):
-            lo, hi = group[0] * C, (group[-1] + 1) * C
-            nc.vector.tensor_tensor(
-                outs[n][:].indirect(dst_list[:, lo // 16 : hi // 16]), ys[group, n][:, : hi - lo], gate_sb[:, lo:hi], MULT
-            )
+        zs = {}
+
+        def weigh(e):
+            z = y_pool.tile([P, NT, C], F32, name="z")
+            weight = gate_sb[:, e * C : (e + 1) * C].unsqueeze(1).to_broadcast([P, NT, C])
+            nc.vector.tensor_tensor(z[:], ys[e][:], weight, MULT)
+            zs[e] = z
+
+        def scatter(e, n):
+            nc.vector.tensor_copy(outs[n][:].indirect(dst_list[:, e * C // 16 : (e + 1) * C // 16]), zs[e][:, n, :])
 
         x_block(0, 0, "s")
         x_block(0, 1, "v")
@@ -193,9 +194,8 @@ def tile_moe_two_lin_gelu_kernel(tc, xT, w, b, gate, offs, dst, out):
             if e == 2:
                 gather_words(1, 1)
                 gather_bytes(1)
-            for group in GROUPS:
-                if e == group[-1]:
-                    for n in range(NT):
-                        scatter(group, n)
-                        if e == E - 1:
-                            nc.sync.dma_start(out=out[n * P : (n + 1) * P, :], in_=outs[n][:])
+            weigh(e)
+            for n in range(NT):
+                scatter(e, n)
+                if e == E - 1:
+                    nc.sync.dma_start(out=out[n * P : (n + 1) * P, :], in_=outs[n][:])

@@ -7,8 +7,8 @@ FLOPS = 2 * K * N * E * C
 
 F32 = mybir.dt.float32
 BF16 = mybir.dt.bfloat16
-U32 = mybir.dt.uint32
 I32 = mybir.dt.int32
+U32 = mybir.dt.uint32
 U16 = mybir.dt.uint16
 U8 = mybir.dt.uint8
 FP8X4 = mybir.dt.float8_e4m3fn_x4
@@ -18,184 +18,185 @@ MULT = mybir.AluOpType.mult
 
 P = 128
 J = 4
-PASSES = 2
-ROWS = 512
+ROWS = P * J
+PASSES = K // ROWS
+SCALE_ROWS = 4
 NT = N // P
-HALF = 512
+SLOTS = E * C
+HALF = SLOTS // 2
+LIST_COLS = 16
+
+X_BLOCK = 256
+X_LOADS = (
+    (0, 0, 256),
+    (0, 256, 256),
+    (0, 512, 512),
+    (1, 0, 512),
+    (1, 512, 256),
+    (1, 768, 256),
+)
+X_ON_VECTOR = ((0, 1), (0, 3), (1, 2))
+W_ON_VECTOR = ((1, 1), (3, 1), (5, 1))
 
 
 def tile_moe_two_lin_gelu_kernel(tc, xT, w, b, gate, offs, dst, out):
     nc = tc.nc
     with ExitStack() as ctx:
         keep = ctx.enter_context(tc.tile_pool(name="keep", bufs=1))
-        xbf_pool = ctx.enter_context(tc.tile_pool(name="xbf", bufs=8))
-        wraw_pool = ctx.enter_context(tc.tile_pool(name="wraw", bufs=14))
-        wbf_pool = ctx.enter_context(tc.tile_pool(name="wbf", bufs=4))
-        wq_pool = ctx.enter_context(tc.tile_pool(name="wq", bufs=4))
-        y_pool = ctx.enter_context(tc.tile_pool(name="y", bufs=4))
+        x_rounded = ctx.enter_context(tc.tile_pool(name="x_rounded", bufs=8))
+        w_arrived = ctx.enter_context(tc.tile_pool(name="w_arrived", bufs=14))
+        w_rounded = ctx.enter_context(tc.tile_pool(name="w_rounded", bufs=4))
+        w_quantised = ctx.enter_context(tc.tile_pool(name="w_quantised", bufs=4))
+        results = ctx.enter_context(tc.tile_pool(name="results", bufs=3 * NT))
         psum = ctx.enter_context(tc.psum_pool(name="psum", bufs=8))
 
-        src_list = keep.tile([P, E * C // 16], U16, name="src_list")
-        dst_list = keep.tile([P, E * C // 16], U16, name="dst_list")
+        src_list = keep.tile([P, SLOTS // LIST_COLS], U16, name="src_list")
+        dst_list = keep.tile([P, SLOTS // LIST_COLS], U16, name="dst_list")
         x_words = [keep.tile([P, T], U32, name=f"x_words{a}", align_bytes=64) for a in range(PASSES)]
         x_bytes = keep.tile([P, T], U8, name="x_bytes", align_bytes=64)
-        gate_sb = keep.tile([P, E * C], F32, name="gate_sb")
+        gate_sb = keep.tile([P, SLOTS], F32, name="gate_sb")
         bias = keep.tile([P, NT, E], F32, name="bias")
-        warm = keep.tile([P, 1], F32, name="warm")
-        warm_out = keep.tile([P, 1], F32, name="warm_out")
-        outs = [keep.tile([P, T], F32, name=f"placed{n}") for n in range(NT)]
-        g_words = [[keep.tile([P, HALF], U32, name=f"g_words{a}{h}", align_bytes=64) for h in range(2)] for a in range(PASSES)]
-        g_bytes = [keep.tile([P, HALF], U8, name=f"g_bytes{h}", align_bytes=64) for h in range(2)]
+        zero = keep.tile([P, 1], F32, name="zero")
+        unused = keep.tile([P, 1], F32, name="unused")
+        placed = [keep.tile([P, T], F32, name=f"placed{n}") for n in range(NT)]
+        slot_words = [
+            [keep.tile([P, HALF], U32, name=f"slot_words{a}_{h}", align_bytes=64) for h in range(2)]
+            for a in range(PASSES)
+        ]
+        slot_bytes = [keep.tile([P, HALF], U8, name=f"slot_bytes{h}", align_bytes=64) for h in range(2)]
+
+        nc.vector.memset(zero[:], 0.0)
+        nc.scalar.activation(unused[:], zero[:], GELU)
+        nc.vector.memset(x_bytes[:].bitcast(I32), 0)
+        nc.scalar.dma_start(out=bias[:], in_=b.rearrange("(n p) e -> p n e", p=P))
 
         x_raw = {}
         w_raw = {}
 
-        def load_x(a, lo, width):
-            raw = keep.tile([P, J, width], F32, name=f"raw_x{a}_{lo}")
-            nc.sync.dma_start(
-                out=raw[:],
-                in_=xT[a * ROWS : (a + 1) * ROWS, lo : lo + width].rearrange("(p j) t -> p j t", j=J),
-            )
-            for b in range(lo // 256, (lo + width) // 256):
-                x_raw[a, b] = raw[:, :, b * 256 - lo : (b + 1) * 256 - lo]
+        def load_x(a, first, tokens):
+            raw = keep.tile([P, J, tokens], F32, name=f"x_raw{a}_{first}")
+            rows = xT[a * ROWS : (a + 1) * ROWS, first : first + tokens]
+            nc.sync.dma_start(out=raw[:], in_=rows.rearrange("(p j) t -> p j t", j=J))
+            for t in range(0, tokens, X_BLOCK):
+                x_raw[a, (first + t) // X_BLOCK] = raw[:, :, t : t + X_BLOCK]
 
         def load_w(e, a):
-            raw = wraw_pool.tile([P, J, N], F32, name="raw_w")
-            nc.sync.dma_start(out=raw[:], in_=w[e, a * ROWS : (a + 1) * ROWS, :].rearrange("(p j) n -> p j n", j=J))
+            raw = w_arrived.tile([P, J, N], F32, name="raw")
+            rows = w[e, a * ROWS : (a + 1) * ROWS, :]
+            nc.sync.dma_start(out=raw[:], in_=rows.rearrange("(p j) n -> p j n", j=J))
             w_raw[e, a] = raw
 
-        nc.vector.memset(warm[:], 0.0)
-        nc.scalar.activation(warm_out[:], warm[:], GELU)
-        nc.vector.memset(x_bytes[:].bitcast(I32), 0)
+        for i, load in enumerate(X_LOADS):
+            load_x(*load)
+            if i == 2:
+                nc.sync.dma_start(src_list[:], offs)
+        for e in range(E):
+            for a in range(PASSES):
+                load_w(e, a)
+            if e == 0:
+                nc.sync.dma_start(dst_list[:], dst)
+            if e == 1:
+                nc.sync.dma_start(out=gate_sb[:], in_=gate[0:P, :])
 
-        load_x(0, 0, 256)
-        load_x(0, 256, 256)
-        load_x(0, 512, 512)
-        nc.sync.dma_start(src_list[:], offs)
-        load_x(1, 0, 512)
-        load_x(1, 512, 256)
-        load_x(1, 768, 256)
-        load_w(0, 0)
-        load_w(0, 1)
-        nc.sync.dma_start(dst_list[:], dst)
-        nc.sync.dma_start(out=bias[:], in_=b.rearrange("(t p) e -> p t e", p=P))
-        load_w(1, 0)
-        load_w(1, 1)
-        nc.sync.dma_start(out=gate_sb[:], in_=gate[0:P, :])
-        load_w(2, 0)
-        load_w(2, 1)
-        load_w(3, 0)
-        load_w(3, 1)
-        load_w(4, 0)
-        load_w(4, 1)
-        load_w(5, 0)
-        load_w(5, 1)
-        load_w(6, 0)
-        load_w(6, 1)
-        load_w(7, 0)
-        load_w(7, 1)
-
-        def interleave(engine, dst_ap, src_ap):
-            o = dst_ap.rearrange("p (c i) j -> p c j i", i=4)
-            i = src_ap.rearrange("p j (c i) -> p c j i", i=4)
-            if engine == "v":
-                nc.vector.tensor_copy(o, i)
+        def interleave(on_vector, grouped, raw):
+            to = grouped.rearrange("p (c i) j -> p c j i", i=4)
+            of = raw.rearrange("p j (c i) -> p c j i", i=4)
+            if on_vector:
+                nc.vector.tensor_copy(to, of)
             else:
-                nc.scalar.activation(o, i, COPY)
+                nc.scalar.activation(to, of, COPY)
 
-        def x_block(a, b, engine):
-            bf = xbf_pool.tile([P, 256, J], BF16, name="bf_x", align_bytes=64)
-            interleave(engine, bf[:], x_raw[a, b])
-            tok = slice(b * 256, (b + 1) * 256)
+        def quantise_tokens(a, block):
+            grouped = x_rounded.tile([P, X_BLOCK, J], BF16, name="grouped_x", align_bytes=64)
+            interleave((a, block) in X_ON_VECTOR, grouped[:], x_raw[a, block])
+            tokens = slice(block * X_BLOCK, (block + 1) * X_BLOCK)
             nc.vector.quantize_mx(
-                out=x_words[a][:, tok].bitcast(FP8X4),
-                scales=x_bytes[J * a : P, tok],
-                in_=bf[:].rearrange("p c j -> p (c j)"),
+                out=x_words[a][:, tokens].bitcast(FP8X4),
+                scales=x_bytes[SCALE_ROWS * a : P, tokens],
+                in_=grouped[:].rearrange("p t j -> p (t j)"),
             )
 
+        def half_of(list_tile, h):
+            cols = HALF // LIST_COLS
+            return list_tile[:, h * cols : (h + 1) * cols]
+
         def gather_words(a, h):
-            nc.vector.tensor_copy(g_words[a][h][:], x_words[a][:].indirect(src_list[:, 32 * h : 32 * (h + 1)]))
+            nc.vector.tensor_copy(slot_words[a][h][:], x_words[a][:].indirect(half_of(src_list, h)))
 
         def gather_bytes(h):
-            nc.vector.tensor_copy(g_bytes[h][:], x_bytes[:].indirect(src_list[:, 32 * h : 32 * (h + 1)]))
+            nc.vector.tensor_copy(slot_bytes[h][:], x_bytes[:].indirect(half_of(src_list, h)))
 
-        w_bf = {}
-        w_q = {}
+        w_grouped = {}
+        w_codes = {}
 
-        def copy_w(e):
-            bf = wbf_pool.tile([P, PASSES * N, J], BF16, name="bf_w", align_bytes=64)
+        def interleave_w(e):
+            grouped = w_rounded.tile([P, PASSES * N, J], BF16, name="grouped_w", align_bytes=64)
             for a in range(PASSES):
-                interleave("v" if (e, a) in ((1, 1), (4, 1), (3, 0),) else "s", bf[:, a * N : (a + 1) * N, :], w_raw[e, a][:])
-            w_bf[e] = bf
+                interleave((e, a) in W_ON_VECTOR, grouped[:, a * N : (a + 1) * N, :], w_raw[e, a][:])
+            w_grouped[e] = grouped
 
-        def quant_w(e):
-            words = wq_pool.tile([P, PASSES * N], U32, name="words_w", align_bytes=64)
-            bytes_w = wq_pool.tile([P, PASSES * N], U8, name="bytes_w", align_bytes=64)
-            flat = w_bf[e][:].rearrange("p c j -> p (c j)")
-            for lo, hi in ((0, 512), (512, 768)):
+        def quantise_w(e):
+            words = w_quantised.tile([P, PASSES * N], U32, name="words", align_bytes=64)
+            scales = w_quantised.tile([P, PASSES * N], U8, name="scales", align_bytes=64)
+            values = w_grouped[e][:].rearrange("p c j -> p (c j)")
+            for lo, hi in ((0, 512), (512, PASSES * N)):
                 nc.vector.quantize_mx(
-                    out=words[:, lo:hi].bitcast(FP8X4), scales=bytes_w[:, lo:hi], in_=flat[:, J * lo : J * hi]
+                    out=words[:, lo:hi].bitcast(FP8X4),
+                    scales=scales[:, lo:hi],
+                    in_=values[:, J * lo : J * hi],
                 )
-            w_q[e] = (words, bytes_w)
+            w_codes[e] = (words, scales)
 
-        ys = {}
+        activated = {}
 
-        def expert(e):
-            words, bytes_w = w_q[e]
-            h, c0 = (e * C) // HALF, (e * C) % HALF
+        def run_expert(e):
+            words, scales = w_codes[e]
+            h, first = divmod(e * C, HALF)
+            slots = slice(first, first + C)
             for n in range(NT):
                 acc = psum.tile([P, C], F32, name="acc")
                 for a in range(PASSES):
-                    col = slice(a * N + n * P, a * N + (n + 1) * P)
+                    channels = slice(a * N + n * P, a * N + (n + 1) * P)
                     nc.tensor.matmul_mx(
                         out=acc[:],
-                        lhsT=words[:, col].bitcast(FP8X4),
-                        lhsT_scale=bytes_w[:, col],
-                        rhs=g_words[a][h][:, c0 : c0 + C].bitcast(FP8X4),
-                        rhs_scale=g_bytes[h][J * a : P, c0 : c0 + C],
+                        lhsT=words[:, channels].bitcast(FP8X4),
+                        lhsT_scale=scales[:, channels],
+                        rhs=slot_words[a][h][:, slots].bitcast(FP8X4),
+                        rhs_scale=slot_bytes[h][SCALE_ROWS * a : P, slots],
                         start=(a == 0),
                         stop=(a == PASSES - 1),
                     )
-                if n == 0:
-                    ys[e] = y_pool.tile([P, NT, C], F32, name="y")
-                nc.scalar.activation(ys[e][:, n, :], acc[:], GELU, bias=bias[:, n, e : e + 1])
-
-        zs = {}
-
-        def weigh(e):
-            z = y_pool.tile([P, NT, C], F32, name="z")
-            weight = gate_sb[:, e * C : (e + 1) * C].unsqueeze(1).to_broadcast([P, NT, C])
-            nc.vector.tensor_tensor(z[:], ys[e][:], weight, MULT)
-            zs[e] = z
+                y = results.tile([P, C], F32, name="y")
+                nc.scalar.activation(y[:], acc[:], GELU, bias=bias[:, n, e : e + 1])
+                activated[e, n] = y
 
         def scatter(e, n):
-            nc.vector.tensor_copy(outs[n][:].indirect(dst_list[:, e * C // 16 : (e + 1) * C // 16]), zs[e][:, n, :])
+            slots = slice(e * C, (e + 1) * C)
+            places = dst_list[:, e * C // LIST_COLS : (e + 1) * C // LIST_COLS]
+            nc.vector.tensor_tensor(
+                placed[n][:].indirect(places), activated[e, n][:], gate_sb[:, slots], MULT
+            )
 
-        x_block(0, 0, "s")
-        x_block(0, 1, "v")
-        x_block(0, 2, "s")
-        x_block(0, 3, "v")
+        for block in range(T // X_BLOCK):
+            quantise_tokens(0, block)
         gather_words(0, 0)
-        x_block(1, 0, "s")
-        x_block(1, 1, "s")
-        x_block(1, 2, "v")
-        x_block(1, 3, "s")
-        copy_w(0)
+        for block in range(T // X_BLOCK):
+            quantise_tokens(1, block)
+        interleave_w(0)
         gather_words(0, 1)
         gather_words(1, 0)
         gather_bytes(0)
-        quant_w(0)
+        quantise_w(0)
+
         for e in range(E):
             if e + 1 < E:
-                copy_w(e + 1)
-            if e + 1 < E:
-                quant_w(e + 1)
-            expert(e)
+                interleave_w(e + 1)
+                quantise_w(e + 1)
+            run_expert(e)
             if e == 2:
                 gather_words(1, 1)
                 gather_bytes(1)
-            weigh(e)
             for n in range(NT):
                 scatter(e, n)
                 if e == E - 1:
-                    nc.sync.dma_start(out=out[n * P : (n + 1) * P, :], in_=outs[n][:])
+                    nc.sync.dma_start(out=out[n * P : (n + 1) * P, :], in_=placed[n][:])

from contextlib import ExitStack

import concourse.mybir as mybir

K, T, E, C, N = 1024, 1024, 8, 128, 384
FLOPS = 2 * K * N * E * C

F32 = mybir.dt.float32
BF16 = mybir.dt.bfloat16
I32 = mybir.dt.int32
U32 = mybir.dt.uint32
U16 = mybir.dt.uint16
U8 = mybir.dt.uint8
FP8X4 = mybir.dt.float8_e4m3fn_x4
COPY = mybir.ActivationFunctionType.Copy
GELU = mybir.ActivationFunctionType.Gelu_apprx_tanh
MULT = mybir.AluOpType.mult

P = 128
J = 4
ROWS = P * J
PASSES = K // ROWS
SCALE_ROWS = 4
NT = N // P
SLOTS = E * C
HALF = SLOTS // 2
LIST_COLS = 16

X_BLOCK = 256
X_LOADS = (
    (0, 0, 256),
    (0, 256, 256),
    (0, 512, 512),
    (1, 0, 512),
    (1, 512, 256),
    (1, 768, 256),
)
X_ON_VECTOR = ((0, 1), (0, 3), (1, 2))
W_ON_VECTOR = ((1, 1), (3, 1), (5, 1))


def tile_moe_two_lin_gelu_kernel(tc, xT, w, b, gate, offs, dst, out):
    nc = tc.nc
    with ExitStack() as ctx:
        keep = ctx.enter_context(tc.tile_pool(name="keep", bufs=1))
        x_rounded = ctx.enter_context(tc.tile_pool(name="x_rounded", bufs=8))
        w_arrived = ctx.enter_context(tc.tile_pool(name="w_arrived", bufs=14))
        w_rounded = ctx.enter_context(tc.tile_pool(name="w_rounded", bufs=4))
        w_quantised = ctx.enter_context(tc.tile_pool(name="w_quantised", bufs=4))
        results = ctx.enter_context(tc.tile_pool(name="results", bufs=3 * NT))
        psum = ctx.enter_context(tc.psum_pool(name="psum", bufs=8))

        src_list = keep.tile([P, SLOTS // LIST_COLS], U16, name="src_list")
        dst_list = keep.tile([P, SLOTS // LIST_COLS], U16, name="dst_list")
        x_words = [keep.tile([P, T], U32, name=f"x_words{a}", align_bytes=64) for a in range(PASSES)]
        x_bytes = keep.tile([P, T], U8, name="x_bytes", align_bytes=64)
        gate_sb = keep.tile([P, SLOTS], F32, name="gate_sb")
        bias = keep.tile([P, NT, E], F32, name="bias")
        zero = keep.tile([P, 1], F32, name="zero")
        unused = keep.tile([P, 1], F32, name="unused")
        placed = [keep.tile([P, T], F32, name=f"placed{n}") for n in range(NT)]
        slot_words = [
            [keep.tile([P, HALF], U32, name=f"slot_words{a}_{h}", align_bytes=64) for h in range(2)]
            for a in range(PASSES)
        ]
        slot_bytes = [keep.tile([P, HALF], U8, name=f"slot_bytes{h}", align_bytes=64) for h in range(2)]

        nc.vector.memset(zero[:], 0.0)
        nc.scalar.activation(unused[:], zero[:], GELU)
        nc.vector.memset(x_bytes[:].bitcast(I32), 0)
        nc.scalar.dma_start(out=bias[:], in_=b.rearrange("(n p) e -> p n e", p=P))

        x_raw = {}
        w_raw = {}

        def load_x(a, first, tokens):
            raw = keep.tile([P, J, tokens], F32, name=f"x_raw{a}_{first}")
            rows = xT[a * ROWS : (a + 1) * ROWS, first : first + tokens]
            nc.sync.dma_start(out=raw[:], in_=rows.rearrange("(p j) t -> p j t", j=J))
            for t in range(0, tokens, X_BLOCK):
                x_raw[a, (first + t) // X_BLOCK] = raw[:, :, t : t + X_BLOCK]

        def load_w(e, a):
            raw = w_arrived.tile([P, J, N], F32, name="raw")
            rows = w[e, a * ROWS : (a + 1) * ROWS, :]
            nc.sync.dma_start(out=raw[:], in_=rows.rearrange("(p j) n -> p j n", j=J))
            w_raw[e, a] = raw

        for i, load in enumerate(X_LOADS):
            load_x(*load)
            if i == 2:
                nc.sync.dma_start(src_list[:], offs)
        for e in range(E):
            for a in range(PASSES):
                load_w(e, a)
            if e == 0:
                nc.sync.dma_start(dst_list[:], dst)
            if e == 1:
                nc.sync.dma_start(out=gate_sb[:], in_=gate[0:P, :])

        def interleave(on_vector, grouped, raw):
            to = grouped.rearrange("p (c i) j -> p c j i", i=4)
            of = raw.rearrange("p j (c i) -> p c j i", i=4)
            if on_vector:
                nc.vector.tensor_copy(to, of)
            else:
                nc.scalar.activation(to, of, COPY)

        def quantise_tokens(a, block):
            grouped = x_rounded.tile([P, X_BLOCK, J], BF16, name="grouped_x", align_bytes=64)
            interleave((a, block) in X_ON_VECTOR, grouped[:], x_raw[a, block])
            tokens = slice(block * X_BLOCK, (block + 1) * X_BLOCK)
            nc.vector.quantize_mx(
                out=x_words[a][:, tokens].bitcast(FP8X4),
                scales=x_bytes[SCALE_ROWS * a : P, tokens],
                in_=grouped[:].rearrange("p t j -> p (t j)"),
            )

        def half_of(list_tile, h):
            cols = HALF // LIST_COLS
            return list_tile[:, h * cols : (h + 1) * cols]

        def gather_words(a, h):
            nc.vector.tensor_copy(slot_words[a][h][:], x_words[a][:].indirect(half_of(src_list, h)))

        def gather_bytes(h):
            nc.vector.tensor_copy(slot_bytes[h][:], x_bytes[:].indirect(half_of(src_list, h)))

        w_grouped = {}
        w_codes = {}

        def interleave_w(e):
            grouped = w_rounded.tile([P, PASSES * N, J], BF16, name="grouped_w", align_bytes=64)
            for a in range(PASSES):
                interleave((e, a) in W_ON_VECTOR, grouped[:, a * N : (a + 1) * N, :], w_raw[e, a][:])
            w_grouped[e] = grouped

        def quantise_w(e):
            words = w_quantised.tile([P, PASSES * N], U32, name="words", align_bytes=64)
            scales = w_quantised.tile([P, PASSES * N], U8, name="scales", align_bytes=64)
            values = w_grouped[e][:].rearrange("p c j -> p (c j)")
            for lo, hi in ((0, 512), (512, PASSES * N)):
                nc.vector.quantize_mx(
                    out=words[:, lo:hi].bitcast(FP8X4),
                    scales=scales[:, lo:hi],
                    in_=values[:, J * lo : J * hi],
                )
            w_codes[e] = (words, scales)

        activated = {}

        def run_expert(e):
            words, scales = w_codes[e]
            h, first = divmod(e * C, HALF)
            slots = slice(first, first + C)
            for n in range(NT):
                acc = psum.tile([P, C], F32, name="acc")
                for a in range(PASSES):
                    channels = slice(a * N + n * P, a * N + (n + 1) * P)
                    nc.tensor.matmul_mx(
                        out=acc[:],
                        lhsT=words[:, channels].bitcast(FP8X4),
                        lhsT_scale=scales[:, channels],
                        rhs=slot_words[a][h][:, slots].bitcast(FP8X4),
                        rhs_scale=slot_bytes[h][SCALE_ROWS * a : P, slots],
                        start=(a == 0),
                        stop=(a == PASSES - 1),
                    )
                y = results.tile([P, C], F32, name="y")
                nc.scalar.activation(y[:], acc[:], GELU, bias=bias[:, n, e : e + 1])
                activated[e, n] = y

        def scatter(e, n):
            slots = slice(e * C, (e + 1) * C)
            places = dst_list[:, e * C // LIST_COLS : (e + 1) * C // LIST_COLS]
            nc.vector.tensor_tensor(
                placed[n][:].indirect(places), activated[e, n][:], gate_sb[:, slots], MULT
            )

        for block in range(T // X_BLOCK):
            quantise_tokens(0, block)
        gather_words(0, 0)
        for block in range(T // X_BLOCK):
            quantise_tokens(1, block)
        interleave_w(0)
        gather_words(0, 1)
        gather_words(1, 0)
        gather_bytes(0)
        quantise_w(0)

        for e in range(E):
            if e + 1 < E:
                interleave_w(e + 1)
                quantise_w(e + 1)
            run_expert(e)
            if e == 2:
                gather_words(1, 1)
                gather_bytes(1)
            for n in range(NT):
                scatter(e, n)
                if e == E - 1:
                    nc.sync.dma_start(out=out[n * P : (n + 1) * P, :], in_=placed[n][:])
